import numpy as np
import ml_dtypes


def mxq(x, axis, fmt="e4m3"):
    dtype, down = {"e4m3": (ml_dtypes.float8_e4m3fn, 7), "e5m2": (ml_dtypes.float8_e5m2, 14)}[fmt]
    v = np.moveaxis(np.asarray(x, np.float32).astype(ml_dtypes.bfloat16).astype(np.float64), axis, -1)
    blocks = v.reshape(v.shape[:-1] + (-1, 32))
    amax = np.abs(blocks).max(-1, keepdims=True)
    byte = np.maximum(np.where(amax > 0, np.frexp(amax)[1] - 1 + 127, 0) - down, 1)
    scale = np.exp2(byte - 127.0)
    codes = (blocks / scale).astype(np.float32).astype(dtype).astype(np.float64)
    return np.moveaxis((codes * scale).reshape(v.shape), -1, axis)


WIDE = False


def mx_kscale(k):
    if not WIDE:
        return np.ones(k)
    levels = np.array([10, -10, 5, -5, 0])
    if k % 512:
        return np.exp2(np.random.permutation(np.resize(levels, k // 32))).repeat(32)
    a = np.empty((k // 512, 16))
    for p in range(k // 512):
        a[p, :8] = np.random.permutation(np.resize(levels, 8))
        for g in range(8):
            far = levels[np.abs(levels - a[p, g]) >= 10]
            a[p, g + 8] = far[np.random.randint(len(far))]
    return np.exp2(a.ravel()).repeat(32)


def f64(x):
    return np.asarray(x).astype(np.float64)


def striped(idx):
    return np.tile(idx.reshape(-1, 16).T, (8, 1)).astype(np.uint16)


def unstriped(offs):
    return offs[:16].T.reshape(-1).astype(np.int64)


E2M1 = np.array([0.0, 0.5, 1.0, 1.5, 2.0, 3.0, 4.0, 6.0, -0.0, -0.5, -1.0, -1.5, -2.0, -3.0, -4.0, -6.0])


def pack_weight(w, fmt):
    k, n = w.shape
    w = f64(np.asarray(w, np.float32).astype(ml_dtypes.bfloat16)).reshape(k // 32, 32, n)
    amax = np.abs(w).max(1)
    if fmt == "e4m3":
        byte = np.frexp(amax)[1] - 1 + 127 - 7
    else:
        mant, ex = np.frexp(amax / 6.0)
        byte = np.where(mant > 0.5, ex, ex - 1) + 127
    byte = np.clip(np.where(amax > 0, byte, 1), 1, 254)
    scaled = (w * np.exp2(127.0 - byte)[:, None, :]).reshape(k, n).astype(np.float32)
    by_word = np.ascontiguousarray(scaled.reshape(k // 512, 128, 4, n).transpose(0, 1, 3, 2))
    if fmt == "e4m3":
        words = by_word.astype(ml_dtypes.float8_e4m3fn).view(np.uint8)
    else:
        c = by_word.astype(ml_dtypes.float4_e2m1fn).view(np.uint8) & 0xF
        words = (c[..., 0::2] | (c[..., 1::2] << 4)).reshape(k // 512, 128, 2 * n)
    return np.ascontiguousarray(words), np.ascontiguousarray(byte.astype(np.uint8).reshape(k // 512, 16, n))


def unpack_weight(words, scales, fmt):
    g, _, n = scales.shape
    words = np.ascontiguousarray(words).reshape(g, 128, n, -1)
    if fmt == "e4m3":
        vals = words.view(ml_dtypes.float8_e4m3fn).astype(np.float64)
    else:
        nib = np.empty((g, 128, n, 4), np.uint8)
        nib[..., 0::2] = words & 0xF
        nib[..., 1::2] = words >> 4
        vals = E2M1[nib]
    vals = vals * np.repeat(np.exp2(scales.astype(np.float64) - 127.0), 8, axis=1)[..., None]
    return vals.transpose(0, 1, 3, 2).reshape(g * 512, n)


def gelu(v):
    return 0.5 * v * (1.0 + np.tanh(np.sqrt(2.0 / np.pi) * (v + 0.044715 * v**3)))


K, L, T, Q, E, C, D = 512, 512, 512, 1024, 4, 128, 256
H, N = 512, 512


def by_expert(wq, xq, C):
    return np.concatenate([wq[e].T @ xq[:, e * C:(e + 1) * C] for e in range(E)], axis=1)


def setup_inputs():
    n = np.random.standard_normal
    s = mx_kscale(K)
    v = mx_kscale(L)
    u = mx_kscale(H)
    slots1, slots2 = np.random.permutation(T)[:E * C], np.random.permutation(Q)[:E * D]
    x = pack_weight(n((K, T)) * s[:, None], "e4m3")
    z = pack_weight(n((L, Q)) * v[:, None], "e4m3")
    return {
        "x_words": x[0],
        "x_scales": x[1],
        "z_words": z[0],
        "z_scales": z[1],
        "w1": (n((E, K, H)) / np.sqrt(K) / s[None, :, None] * u).astype(np.float32),
        "wz": (n((E, L, H)) / np.sqrt(L) / v[None, :, None] * u).astype(np.float32),
        "w2": (n((E, H, N)) / np.sqrt(H) / u[None, :, None]).astype(np.float32),
        "gate1": (np.tile(np.random.uniform(0.2, 1.0, E * C), (128, 1))).astype(np.float32),
        "gate2": (np.tile(np.random.uniform(0.2, 1.0, E * D), (128, 1))).astype(np.float32),
        "offs": striped(slots1),
        "offs2": striped(slots2),
    }


def reference(x_words, x_scales, z_words, z_scales, w1, wz, w2, gate1, gate2, offs, offs2):
    w1q = mxq(f64(w1), 1, "e4m3")
    wzq = mxq(f64(wz), 1, "e4m3")
    w2q = mxq(f64(w2), 1, "e4m3")
    idx, idx2 = unstriped(offs), unstriped(offs2)
    xq = unpack_weight(x_words, x_scales, "e4m3")[:, idx]
    zq = unpack_weight(z_words, z_scales, "e4m3")[:, idx2]
    h = gelu(by_expert(w1q, xq, C))
    p = gelu(by_expert(wzq, zq, D))
    out = np.zeros((N, T + Q))
    out[:, idx] = f64(gate1[:1]) * by_expert(w2q, mxq(h, 0, "e4m3"), C)
    out[:, T + idx2] = f64(gate2[:1]) * by_expert(w2q, mxq(p, 0, "e4m3"), D)
    return out

@@ -1,0 +1,197 @@
+from contextlib import ExitStack
+
+import concourse.mybir as mybir
+
+K, T, Q, E, C, D = 512, 512, 1024, 4, 128, 256
+H, N = 512, 512
+FLOPS = 2 * 2 * 512 * 512 * (E * C + E * D)
+
+F32 = mybir.dt.float32
+BF16 = mybir.dt.bfloat16
+I32 = mybir.dt.int32
+U32 = mybir.dt.uint32
+U16 = mybir.dt.uint16
+U8 = mybir.dt.uint8
+FP8X4 = mybir.dt.float8_e4m3fn_x4
+MULT = mybir.AluOpType.mult
+GELU = mybir.ActivationFunctionType.Gelu_apprx_tanh
+
+P = 128
+PACK = 4
+HALF = 256
+
+
+def tile_moe_mmo_gelu_kernel(
+    tc, x_words, x_scales, z_words, z_scales, w1, wz, w2, gate1, gate2, offs, offs2, out
+):
+    nc = tc.nc
+    with ExitStack() as ctx:
+        keep = ctx.enter_context(tc.tile_pool(name="keep", bufs=1))
+        ring = ctx.enter_context(tc.tile_pool(name="ring", bufs=4))
+        psum = ctx.enter_context(tc.psum_pool(name="psum", bufs=4))
+
+        def load_table(name, words, scales, lst, width, scale_queue):
+            offsets = keep.tile([P, width // 16], U16, name=name + "_offsets")
+            table = keep.tile([P, width], I32, name=name + "_table", align_bytes=64)
+            plane = keep.tile([P, width], U8, name=name + "_plane", align_bytes=64)
+            nc.vector.memset(plane[:].bitcast(I32), 0)
+            nc.sync.dma_start(table[:], words[0].rearrange("p t d -> p (t d)").bitcast(I32))
+            nc.sync.dma_start(offsets[:], lst)
+            for r in range(4):
+                scale_queue.dma_start(plane[r:P:32, :].bitcast(I32), scales[0, r:16:4, :].bitcast(I32))
+            return offsets, table, plane
+
+        def gather(name, offsets, table, plane, width, piece):
+            codes = keep.tile([P, width], U32, name=name + "_codes", align_bytes=64)
+            bytes_ = keep.tile([P, width], U8, name=name + "_bytes", align_bytes=64)
+            for s0 in range(0, width, piece):
+                lst = offsets[:, s0 // 16 : (s0 + piece) // 16]
+                nc.vector.tensor_copy(codes[:, s0 : s0 + piece], table[:].bitcast(U32).indirect(lst))
+                nc.vector.tensor_copy(bytes_[:, s0 : s0 + piece], plane[:].indirect(lst))
+            return codes, bytes_
+
+        def load_half(name, w, h):
+            raw = keep.tile([P, PACK, HALF], F32, name="%s_raw%d" % (name, h))
+            nc.sync.dma_start(raw[:], w[:, h * HALF : (h + 1) * HALF].rearrange("(p j) c -> p j c", j=PACK))
+            return raw[:]
+
+        def load_whole(name, w):
+            raw = keep.tile([P, PACK, 2 * HALF], F32, name=name + "_raw")
+            nc.sync.dma_start(raw[:], w.rearrange("(p j) c -> p j c", j=PACK))
+            return [raw[:, :, h * HALF : (h + 1) * HALF] for h in range(2)]
+
+        def load_gate(name, gate, width):
+            g = keep.tile([P, width], F32, name=name)
+            nc.sync.dma_start(g[:], gate)
+            return g
+
+        z_offsets, z_table, z_plane = load_table("z", z_words, z_scales, offs2, Q, nc.scalar)
+        first_raw = {0: [load_half("wz0", wz[0], h) for h in range(2)]}
+        second_raw = {0: [load_half("w20", w2[0], 0)]}
+        first_raw[1] = [load_half("wz1", wz[1], 0)]
+        x_offsets, x_table, x_plane = load_table("x", x_words, x_scales, offs, T, nc.sync)
+        first_raw[1].append(load_half("wz1", wz[1], 1))
+        z_gate0 = load_gate("z_gate0", gate2[:, 0:D], D)
+        second_raw[0].append(load_half("w20", w2[0], 1))
+        z_gate1 = load_gate("z_gate1", gate2[:, D:Q], Q - D)
+        z_gate = [z_gate0[:]] + [z_gate1[:, e * D : (e + 1) * D] for e in range(E - 1)]
+        second_raw[1] = load_whole("w21", w2[1])
+        for e in range(2, E):
+            first_raw[e] = load_whole("wz%d" % e, wz[e])
+            second_raw[e] = load_whole("w2%d" % e, w2[e])
+        x_gate_all = load_gate("x_gate", gate1, T)
+        x_gate = [x_gate_all[:, e * C : (e + 1) * C] for e in range(E)]
+        for e in range(E):
+            first_raw[E + e] = load_whole("w1%d" % e, w1[e])
+
+        z_codes, z_bytes = gather("z", z_offsets, z_table, z_plane, Q, D)
+        x_codes, x_bytes = gather("x", x_offsets, x_table, x_plane, T, 2 * C)
+
+        z_win = [keep.tile([P, Q], F32, name="z_win%d" % b) for b in range(4)]
+        x_win = [keep.tile([P, T], F32, name="x_win%d" % b) for b in range(4)]
+
+        def unit(u):
+            if u < E:
+                return u, D, z_codes, z_bytes, z_offsets, z_gate, z_win, T
+            return u - E, C, x_codes, x_bytes, x_offsets, x_gate, x_win, 0
+
+        first_q = {}
+        second_q = {}
+        hidden_q = {}
+
+        def quantise_first(u):
+            grouped = ring.tile([P, PACK, P, PACK], BF16, name="first_grouped", align_bytes=64, bufs=3)
+            for h in range(2):
+                nc.scalar.copy(
+                    grouped[:, :, h * 64 : (h + 1) * 64, :].rearrange("p t m j -> p m j t"),
+                    first_raw[u][h].rearrange("p j (m t) -> p m j t", t=PACK),
+                )
+            codes = ring.tile([P, H], U32, name="first_codes", align_bytes=64)
+            scales = ring.tile([P, H], U8, name="first_scales", align_bytes=64)
+            nc.vector.quantize_mx(out=codes[:].bitcast(FP8X4), scales=scales[:], in_=grouped[:].rearrange("p t m j -> p (t m j)"))
+            first_q[u] = (codes, scales)
+
+        def quantise_second(e, h):
+            grouped = ring.tile([P, HALF, PACK], BF16, name="second_grouped", align_bytes=64)
+            nc.scalar.copy(
+                grouped[:].rearrange("p (c i) j -> p c j i", i=4),
+                second_raw[e][h].rearrange("p j (c i) -> p c j i", i=4),
+            )
+            codes = keep.tile([P, HALF], U32, name="second_codes%d_%d" % (e, h), align_bytes=64)
+            scales = keep.tile([P, HALF], U8, name="second_scales%d_%d" % (e, h), align_bytes=64)
+            nc.vector.quantize_mx(out=codes[:].bitcast(FP8X4), scales=scales[:], in_=grouped[:].rearrange("p c j -> p (c j)"))
+            second_q[(e, h)] = (codes, scales)
+
+        def hidden(u):
+            e, slots, codes, bytes_, offsets, gate, win, col0 = unit(u)
+            w_codes, w_scales = first_q[u]
+            grouped = ring.tile([P, slots, PACK], BF16, name="hidden_grouped", align_bytes=64, bufs=3)
+            for s0 in range(0, slots, P):
+                acc = psum.tile([P, PACK, P], F32, name="first_acc")
+                cols = slice(e * slots + s0, e * slots + s0 + P)
+                for t in range(PACK):
+                    nc.tensor.matmul_mx(
+                        out=acc[:, t, :],
+                        lhsT=w_codes[:, t * P : (t + 1) * P].bitcast(FP8X4),
+                        lhsT_scale=w_scales[:, t * P : (t + 1) * P],
+                        rhs=codes[:, cols].bitcast(FP8X4),
+                        rhs_scale=bytes_[:, cols],
+                        start=True,
+                        stop=True,
+                    )
+                nc.scalar.activation(grouped[:, s0 : s0 + P, :], acc[:].rearrange("p t s -> p s t"), GELU)
+            h_codes = ring.tile([P, slots], U32, name="hidden_codes", align_bytes=64)
+            h_scales = ring.tile([P, slots], U8, name="hidden_scales", align_bytes=64)
+            nc.vector.quantize_mx(out=h_codes[:].bitcast(FP8X4), scales=h_scales[:], in_=grouped[:].rearrange("p s t -> p (s t)"))
+            hidden_q[u] = (h_codes, h_scales)
+
+        def results(u, h):
+            e, slots, codes, bytes_, offsets, gate, win, col0 = unit(u)
+            h_codes, h_scales = hidden_q[u]
+            w_codes, w_scales = second_q[(e, h)]
+            acc = psum.tile([P, 2, slots], F32, name="second_acc")
+            for b in range(2):
+                nc.tensor.matmul_mx(
+                    out=acc[:, b, :],
+                    lhsT=w_codes[:, b * P : (b + 1) * P].bitcast(FP8X4),
+                    lhsT_scale=w_scales[:, b * P : (b + 1) * P],
+                    rhs=h_codes[:].bitcast(FP8X4),
+                    rhs_scale=h_scales[:],
+                    start=True,
+                    stop=True,
+                )
+            res = ring.tile([P, 2 * slots], F32, name="res")
+            nc.scalar.copy(res[:], acc[:].rearrange("p b s -> p (b s)"))
+            lst = offsets[:, e * slots // 16 : (e + 1) * slots // 16]
+            for b in range(2):
+                nb = 2 * h + b
+                nc.vector.tensor_tensor(
+                    win[nb][:].indirect(lst), res[:, b * slots : (b + 1) * slots], gate[e], MULT
+                )
+                if e == E - 1:
+                    nc.sync.dma_start(out[nb * P : (nb + 1) * P, col0 : col0 + E * slots], win[nb][:])
+
+        quantise_first(0)
+        quantise_second(0, 0)
+        hidden(0)
+        quantise_first(1)
+        for u in range(2 * E):
+            results(u, 0)
+            if u == 0:
+                quantise_second(0, 1)
+            if u + 1 < 2 * E:
+                hidden(u + 1)
+            if u + 1 < E:
+                quantise_second(u + 1, 0)
+                results(u, 1)
+                quantise_first(u + 2)
+                quantise_second(u + 1, 1)
+            elif u == E - 1:
+                quantise_first(u + 2)
+                results(u, 1)
+                quantise_first(u + 3)
+            elif u == E:
+                quantise_first(u + 3)
+                results(u, 1)
+            else:
+                results(u, 1)

@@ -19,6 +19,8 @@ GELU = mybir.ActivationFunctionType.Gelu_apprx_tanh
 P = 128
 PACK = 4
 HALF = 256
+SLOT = 4096
+BANK = 2048
 
 
 def tile_moe_mmo_gelu_kernel(
@@ -27,8 +29,9 @@ def tile_moe_mmo_gelu_kernel(
     nc = tc.nc
     with ExitStack() as ctx:
         keep = ctx.enter_context(tc.tile_pool(name="keep", bufs=1))
+        stage = ctx.enter_context(tc.tile_pool(name="stage", bufs=1))
         ring = ctx.enter_context(tc.tile_pool(name="ring", bufs=4))
-        psum = ctx.enter_context(tc.psum_pool(name="psum", bufs=4))
+        psum = ctx.enter_context(tc.psum_pool(name="psum", bufs=1))
 
         def load_table(name, words, scales, lst, width, scale_queue):
             offsets = keep.tile([P, width // 16], U16, name=name + "_offsets")
@@ -41,70 +44,83 @@ def tile_moe_mmo_gelu_kernel(
                 scale_queue.dma_start(plane[r:P:32, :].bitcast(I32), scales[0, r:16:4, :].bitcast(I32))
             return offsets, table, plane
 
-        def gather(name, offsets, table, plane, width, piece):
-            codes = keep.tile([P, width], U32, name=name + "_codes", align_bytes=64)
-            bytes_ = keep.tile([P, width], U8, name=name + "_bytes", align_bytes=64)
-            for s0 in range(0, width, piece):
-                lst = offsets[:, s0 // 16 : (s0 + piece) // 16]
-                nc.vector.tensor_copy(codes[:, s0 : s0 + piece], table[:].bitcast(U32).indirect(lst))
-                nc.vector.tensor_copy(bytes_[:, s0 : s0 + piece], plane[:].indirect(lst))
-            return codes, bytes_
+        raw = {}
+        place = {}
 
-        def load_half(name, w, h):
-            raw = keep.tile([P, PACK, HALF], F32, name="%s_raw%d" % (name, h))
-            nc.sync.dma_start(raw[:], w[:, h * HALF : (h + 1) * HALF].rearrange("(p j) c -> p j c", j=PACK))
-            return raw[:]
+        def load_half(key, w, h):
+            place[(key, h)] = len(place) * SLOT
+            t = stage.tile([P, PACK, HALF], F32, name="raw_%s%d" % (key, h), offset=place[(key, h)])
+            nc.sync.dma_start(t[:], w[:, h * HALF : (h + 1) * HALF].rearrange("(p j) c -> p j c", j=PACK))
+            raw[(key, h)] = t[:]
 
-        def load_whole(name, w):
-            raw = keep.tile([P, PACK, 2 * HALF], F32, name=name + "_raw")
-            nc.sync.dma_start(raw[:], w.rearrange("(p j) c -> p j c", j=PACK))
-            return [raw[:, :, h * HALF : (h + 1) * HALF] for h in range(2)]
+        def load_whole(key, w):
+            for h in range(2):
+                place[(key, h)] = len(place) * SLOT
+            t = stage.tile([P, PACK, 2 * HALF], F32, name="raw_" + key, offset=place[(key, 0)])
+            nc.sync.dma_start(t[:], w.rearrange("(p j) c -> p j c", j=PACK))
+            for h in range(2):
+                raw[(key, h)] = t[:, :, h * HALF : (h + 1) * HALF]
 
         def load_gate(name, gate, width):
             g = keep.tile([P, width], F32, name=name)
             nc.sync.dma_start(g[:], gate)
             return g
 
-        z_offsets, z_table, z_plane = load_table("z", z_words, z_scales, offs2, Q, nc.scalar)
-        first_raw = {0: [load_half("wz0", wz[0], h) for h in range(2)]}
-        second_raw = {0: [load_half("w20", w2[0], 0)]}
-        first_raw[1] = [load_half("wz1", wz[1], 0)]
-        x_offsets, x_table, x_plane = load_table("x", x_words, x_scales, offs, T, nc.sync)
-        first_raw[1].append(load_half("wz1", wz[1], 1))
-        z_gate0 = load_gate("z_gate0", gate2[:, 0:D], D)
-        second_raw[0].append(load_half("w20", w2[0], 1))
-        z_gate1 = load_gate("z_gate1", gate2[:, D:Q], Q - D)
-        z_gate = [z_gate0[:]] + [z_gate1[:, e * D : (e + 1) * D] for e in range(E - 1)]
-        second_raw[1] = load_whole("w21", w2[1])
-        for e in range(2, E):
-            first_raw[e] = load_whole("wz%d" % e, wz[e])
-            second_raw[e] = load_whole("w2%d" % e, w2[e])
-        x_gate_all = load_gate("x_gate", gate1, T)
-        x_gate = [x_gate_all[:, e * C : (e + 1) * C] for e in range(E)]
-        for e in range(E):
-            first_raw[E + e] = load_whole("w1%d" % e, w1[e])
+        def first_w(u):
+            return wz[u] if u < E else w1[u - E]
 
-        z_codes, z_bytes = gather("z", z_offsets, z_table, z_plane, Q, D)
-        x_codes, x_bytes = gather("x", x_offsets, x_table, x_plane, T, 2 * C)
+        z_lists = load_table("z", z_words, z_scales, offs2, Q, nc.scalar)
+        load_half("first0", wz[0], 0)
+        load_half("first0", wz[0], 1)
+        load_half("second0", w2[0], 0)
+        x_lists = load_table("x", x_words, x_scales, offs, T, nc.sync)
+        load_half("first1", wz[1], 0)
+        load_half("first1", wz[1], 1)
+        load_half("second0", w2[0], 1)
+        gates = [load_gate("z_gate0", gate2[:, 0:D], D)[:]]
+        for e in range(1, E):
+            load_half("second%d" % e, w2[e], 0)
+            load_whole("first%d" % (e + 1), first_w(e + 1))
+            gates.append(load_gate("z_gate%d" % e, gate2[:, e * D : (e + 1) * D], D)[:])
+            load_half("second%d" % e, w2[e], 1)
+        load_whole("first5", w1[1])
+        load_whole("first6", w1[2])
+        x_gate = load_gate("x_gate", gate1, T)
+        gates.extend([x_gate[:, e * C : (e + 1) * C] for e in range(E)])
+        load_whole("first7", w1[3])
 
         z_win = [keep.tile([P, Q], F32, name="z_win%d" % b) for b in range(4)]
         x_win = [keep.tile([P, T], F32, name="x_win%d" % b) for b in range(4)]
 
-        def unit(u):
-            if u < E:
-                return u, D, z_codes, z_bytes, z_offsets, z_gate, z_win, T
-            return u - E, C, x_codes, x_bytes, x_offsets, x_gate, x_win, 0
-
+        tokens = {}
         first_q = {}
         second_q = {}
         hidden_q = {}
+
+        def new_tile(shape, dtype, name, at):
+            if at is None:
+                return keep.tile(shape, dtype, name=name, align_bytes=64)
+            return stage.tile(shape, dtype, name=name, align_bytes=64, offset=at)
+
+        def gather(units, at):
+            offsets, table, plane = z_lists if units[0] < E else x_lists
+            slots = D if units[0] < E else C
+            n = slots * len(units)
+            s0 = (units[0] % E) * slots
+            codes = new_tile([P, n], U32, "codes%d" % units[0], at)
+            bytes_ = new_tile([P, n], U8, "bytes%d" % units[0], None if at is None else at + 4 * n)
+            lst = offsets[:, s0 // 16 : (s0 + n) // 16]
+            nc.vector.tensor_copy(codes[:], table[:].bitcast(U32).indirect(lst))
+            nc.vector.tensor_copy(bytes_[:], plane[:].indirect(lst))
+            for i, u in enumerate(units):
+                tokens[u] = (codes[:, i * slots : (i + 1) * slots], bytes_[:, i * slots : (i + 1) * slots])
 
         def quantise_first(u):
             grouped = ring.tile([P, PACK, P, PACK], BF16, name="first_grouped", align_bytes=64, bufs=3)
             for h in range(2):
                 nc.scalar.copy(
                     grouped[:, :, h * 64 : (h + 1) * 64, :].rearrange("p t m j -> p m j t"),
-                    first_raw[u][h].rearrange("p j (m t) -> p m j t", t=PACK),
+                    raw[("first%d" % u, h)].rearrange("p j (m t) -> p m j t", t=PACK),
                 )
             codes = ring.tile([P, H], U32, name="first_codes", align_bytes=64)
             scales = ring.tile([P, H], U8, name="first_scales", align_bytes=64)
@@ -115,20 +131,21 @@ def tile_moe_mmo_gelu_kernel(
             grouped = ring.tile([P, HALF, PACK], BF16, name="second_grouped", align_bytes=64)
             nc.scalar.copy(
                 grouped[:].rearrange("p (c i) j -> p c j i", i=4),
-                second_raw[e][h].rearrange("p j (c i) -> p c j i", i=4),
+                raw[("second%d" % e, h)].rearrange("p j (c i) -> p c j i", i=4),
             )
             codes = keep.tile([P, HALF], U32, name="second_codes%d_%d" % (e, h), align_bytes=64)
             scales = keep.tile([P, HALF], U8, name="second_scales%d_%d" % (e, h), align_bytes=64)
             nc.vector.quantize_mx(out=codes[:].bitcast(FP8X4), scales=scales[:], in_=grouped[:].rearrange("p c j -> p (c j)"))
             second_q[(e, h)] = (codes, scales)
 
-        def hidden(u):
-            e, slots, codes, bytes_, offsets, gate, win, col0 = unit(u)
+        def hidden(u, banks, at):
+            slots = D if u < E else C
+            codes, bytes_ = tokens[u]
             w_codes, w_scales = first_q[u]
-            grouped = ring.tile([P, slots, PACK], BF16, name="hidden_grouped", align_bytes=64, bufs=3)
-            for s0 in range(0, slots, P):
-                acc = psum.tile([P, PACK, P], F32, name="first_acc")
-                cols = slice(e * slots + s0, e * slots + s0 + P)
+            grouped = new_tile([P, slots, PACK], BF16, "hidden_grouped%d" % u, at)
+            for g in range(slots // P):
+                acc = psum.tile([P, PACK, P], F32, name="first_acc%d_%d" % (u, g), offset=banks[g] * BANK)
+                cols = slice(g * P, (g + 1) * P)
                 for t in range(PACK):
                     nc.tensor.matmul_mx(
                         out=acc[:, t, :],
@@ -139,59 +156,66 @@ def tile_moe_mmo_gelu_kernel(
                         start=True,
                         stop=True,
                     )
-                nc.scalar.activation(grouped[:, s0 : s0 + P, :], acc[:].rearrange("p t s -> p s t"), GELU)
+                nc.scalar.activation(grouped[:, cols, :], acc[:].rearrange("p t s -> p s t"), GELU)
             h_codes = ring.tile([P, slots], U32, name="hidden_codes", align_bytes=64)
             h_scales = ring.tile([P, slots], U8, name="hidden_scales", align_bytes=64)
             nc.vector.quantize_mx(out=h_codes[:].bitcast(FP8X4), scales=h_scales[:], in_=grouped[:].rearrange("p s t -> p (s t)"))
             hidden_q[u] = (h_codes, h_scales)
 
-        def results(u, h):
-            e, slots, codes, bytes_, offsets, gate, win, col0 = unit(u)
+        def results(u, blocks, bank, at):
+            e = u % E
+            slots = D if u < E else C
+            offsets = (z_lists if u < E else x_lists)[0]
+            win = z_win if u < E else x_win
+            col0 = T if u < E else 0
             h_codes, h_scales = hidden_q[u]
-            w_codes, w_scales = second_q[(e, h)]
-            acc = psum.tile([P, 2, slots], F32, name="second_acc")
-            for b in range(2):
+            acc = psum.tile([P, len(blocks), slots], F32, name="second_acc%d_%d" % (u, blocks[0]), offset=bank * BANK)
+            for i, nb in enumerate(blocks):
+                w_codes, w_scales = second_q[(e, nb // 2)]
+                cols = slice((nb % 2) * P, (nb % 2 + 1) * P)
                 nc.tensor.matmul_mx(
-                    out=acc[:, b, :],
-                    lhsT=w_codes[:, b * P : (b + 1) * P].bitcast(FP8X4),
-                    lhsT_scale=w_scales[:, b * P : (b + 1) * P],
+                    out=acc[:, i, :],
+                    lhsT=w_codes[:, cols].bitcast(FP8X4),
+                    lhsT_scale=w_scales[:, cols],
                     rhs=h_codes[:].bitcast(FP8X4),
                     rhs_scale=h_scales[:],
                     start=True,
                     stop=True,
                 )
-            res = ring.tile([P, 2 * slots], F32, name="res")
+            res = new_tile([P, len(blocks) * slots], F32, "res%d_%d" % (u, blocks[0]), at)
             nc.scalar.copy(res[:], acc[:].rearrange("p b s -> p (b s)"))
             lst = offsets[:, e * slots // 16 : (e + 1) * slots // 16]
-            for b in range(2):
-                nb = 2 * h + b
-                nc.vector.tensor_tensor(
-                    win[nb][:].indirect(lst), res[:, b * slots : (b + 1) * slots], gate[e], MULT
-                )
+            for i, nb in enumerate(blocks):
+                nc.vector.tensor_tensor(win[nb][:].indirect(lst), res[:, i * slots : (i + 1) * slots], gates[u], MULT)
                 if e == E - 1:
                     nc.sync.dma_start(out[nb * P : (nb + 1) * P, col0 : col0 + E * slots], win[nb][:])
 
+        gather([0], None)
+        gather([1, 2], None)
         quantise_first(0)
+        gather([3], place[("first0", 1)])
+        gather([4, 5], place[("first0", 1)] + SLOT // 2)
         quantise_second(0, 0)
-        hidden(0)
+        hidden(0, (0, 1), None)
         quantise_first(1)
-        for u in range(2 * E):
-            results(u, 0)
-            if u == 0:
-                quantise_second(0, 1)
-            if u + 1 < 2 * E:
-                hidden(u + 1)
+        gather([6, 7], place[("first1", 0)])
+        quantise_second(0, 1)
+        for u in range(E):
+            behind = place[("second%d" % u, 1)]
+            results(u, (0, 1), 4 + 2 * (u % 2), behind)
+            hidden(u + 1, (2, 3) if u % 2 == 0 else (0, 1), behind + SLOT // 2)
             if u + 1 < E:
                 quantise_second(u + 1, 0)
-                results(u, 1)
+                results(u, (2, 3), 5 + 2 * (u % 2), place[("second%d" % (u + 1), 0)])
                 quantise_first(u + 2)
                 quantise_second(u + 1, 1)
-            elif u == E - 1:
-                quantise_first(u + 2)
-                results(u, 1)
-                quantise_first(u + 3)
-            elif u == E:
-                quantise_first(u + 3)
-                results(u, 1)
             else:
-                results(u, 1)
+                quantise_first(u + 2)
+                results(u, (2, 3), 5 + 2 * (u % 2), place[("first%d" % (u + 2), 0)])
+        for u in range(E, 2 * E):
+            bank = 2 * ((u + 1) % 2)
+            if u + 1 < 2 * E:
+                hidden(u + 1, (bank,), None)
+            if u + 2 < 2 * E:
+                quantise_first(u + 2)
+            results(u, (0, 1, 2, 3), bank, place[("first%d" % (u + 2), 0)] if u + 2 < 2 * E else None)

@@ -38,8 +38,8 @@ def tile_moe_mmo_gelu_kernel(
             table = keep.tile([P, width], I32, name=name + "_table", align_bytes=64)
             plane = keep.tile([P, width], U8, name=name + "_plane", align_bytes=64)
             nc.vector.memset(plane[:].bitcast(I32), 0)
-            nc.sync.dma_start(table[:], words[0].rearrange("p t d -> p (t d)").bitcast(I32))
             nc.sync.dma_start(offsets[:], lst)
+            nc.sync.dma_start(table[:], words[0].rearrange("p t d -> p (t d)").bitcast(I32))
             for r in range(4):
                 scale_queue.dma_start(plane[r:P:32, :].bitcast(I32), scales[0, r:16:4, :].bitcast(I32))
             return offsets, table, plane
@@ -72,9 +72,9 @@ def tile_moe_mmo_gelu_kernel(
         z_lists = load_table("z", z_words, z_scales, offs2, Q, nc.scalar)
         load_half("first0", wz[0], 0)
         load_half("first0", wz[0], 1)
+        load_half("first1", wz[1], 0)
         load_half("second0", w2[0], 0)
         x_lists = load_table("x", x_words, x_scales, offs, T, nc.sync)
-        load_half("first1", wz[1], 0)
         load_half("first1", wz[1], 1)
         load_half("second0", w2[0], 1)
         gates = [load_gate("z_gate0", gate2[:, 0:D], D)[:]]
@@ -102,21 +102,22 @@ def tile_moe_mmo_gelu_kernel(
                 return keep.tile(shape, dtype, name=name, align_bytes=64)
             return stage.tile(shape, dtype, name=name, align_bytes=64, offset=at)
 
-        def gather(units, at):
+        def gather(units, sort, at):
             offsets, table, plane = z_lists if units[0] < E else x_lists
+            window, dtype = (table[:].bitcast(U32), U32) if sort == 0 else (plane[:], U8)
             slots = D if units[0] < E else C
             n = slots * len(units)
             s0 = (units[0] % E) * slots
-            codes = new_tile([P, n], U32, "codes%d" % units[0], at)
-            bytes_ = new_tile([P, n], U8, "bytes%d" % units[0], None if at is None else at + 4 * n)
-            lst = offsets[:, s0 // 16 : (s0 + n) // 16]
-            nc.vector.tensor_copy(codes[:], table[:].bitcast(U32).indirect(lst))
-            nc.vector.tensor_copy(bytes_[:], plane[:].indirect(lst))
+            got = new_tile([P, n], dtype, "gathered%d_%d" % (sort, units[0]), at)
+            nc.vector.tensor_copy(got[:], window.indirect(offsets[:, s0 // 16 : (s0 + n) // 16]))
             for i, u in enumerate(units):
-                tokens[u] = (codes[:, i * slots : (i + 1) * slots], bytes_[:, i * slots : (i + 1) * slots])
+                tokens[(u, sort)] = got[:, i * slots : (i + 1) * slots]
 
-        def quantise_first(u):
-            grouped = ring.tile([P, PACK, P, PACK], BF16, name="first_grouped", align_bytes=64, bufs=3)
+        def quantise_first(u, at=None):
+            if at is None:
+                grouped = ring.tile([P, PACK, P, PACK], BF16, name="first_grouped", align_bytes=64, bufs=3)
+            else:
+                grouped = new_tile([P, PACK, P, PACK], BF16, "first_grouped_at", at)
             for h in range(2):
                 nc.scalar.copy(
                     grouped[:, :, h * 64 : (h + 1) * 64, :].rearrange("p t m j -> p m j t"),
@@ -127,9 +128,12 @@ def tile_moe_mmo_gelu_kernel(
             nc.vector.quantize_mx(out=codes[:].bitcast(FP8X4), scales=scales[:], in_=grouped[:].rearrange("p t m j -> p (t m j)"))
             first_q[u] = (codes, scales)
 
-        def quantise_second(e, h):
-            grouped = ring.tile([P, HALF, PACK], BF16, name="second_grouped", align_bytes=64)
-            nc.scalar.copy(
+        def quantise_second(e, h, cast=nc.scalar.copy, at=None):
+            if at is None:
+                grouped = ring.tile([P, HALF, PACK], BF16, name="second_grouped", align_bytes=64)
+            else:
+                grouped = new_tile([P, HALF, PACK], BF16, "second_grouped_at", at)
+            cast(
                 grouped[:].rearrange("p (c i) j -> p c j i", i=4),
                 raw[("second%d" % e, h)].rearrange("p j (c i) -> p c j i", i=4),
             )
@@ -140,7 +144,7 @@ def tile_moe_mmo_gelu_kernel(
 
         def hidden(u, banks, at):
             slots = D if u < E else C
-            codes, bytes_ = tokens[u]
+            codes, bytes_ = tokens[(u, 0)], tokens[(u, 1)]
             w_codes, w_scales = first_q[u]
             grouped = new_tile([P, slots, PACK], BF16, "hidden_grouped%d" % u, at)
             for g in range(slots // P):
@@ -190,15 +194,18 @@ def tile_moe_mmo_gelu_kernel(
                 if e == E - 1:
                     nc.sync.dma_start(out[nb * P : (nb + 1) * P, col0 : col0 + E * slots], win[nb][:])
 
-        gather([0], None)
-        gather([1, 2], None)
-        quantise_first(0)
-        gather([3], place[("first0", 1)])
-        gather([4, 5], place[("first0", 1)] + SLOT // 2)
-        quantise_second(0, 0)
+        gather([0, 1], 0, None)
+        gather([2, 3], 0, None)
+        gather([0, 1, 2], 1, None)
+        quantise_first(0, len(place) * SLOT)
+        gather([3], 1, place[("first0", 1)])
+        quantise_second(0, 0, nc.vector.tensor_copy, len(place) * SLOT)
+        gather([4, 5], 0, place[("first0", 1)] + 1024)
+        gather([4, 5], 1, place[("first0", 1)] + 2048)
         hidden(0, (0, 1), None)
         quantise_first(1)
-        gather([6, 7], place[("first1", 0)])
+        gather([6, 7], 0, place[("first1", 1)])
+        gather([6, 7], 1, place[("first1", 1)] + 1024)
         quantise_second(0, 1)
         for u in range(E):
             behind = place[("second%d" % u, 1)]

@@ -2,9 +2,9 @@ from contextlib import ExitStack
 
 import concourse.mybir as mybir
 
-K, T, Q, E, C, D = 512, 512, 1024, 4, 128, 256
-H, N = 512, 512
-FLOPS = 2 * 2 * 512 * 512 * (E * C + E * D)
+T, Q, E, C, D = 512, 1024, 4, 128, 256
+H = 512
+FLOPS = 2 * 2 * 512 * 512 * (T + Q)
 
 F32 = mybir.dt.float32
 BF16 = mybir.dt.bfloat16
@@ -19,8 +19,11 @@ GELU = mybir.ActivationFunctionType.Gelu_apprx_tanh
 P = 128
 PACK = 4
 HALF = 256
-SLOT = 4096
+SLOT = PACK * HALF * 4
 BANK = 2048
+BLOCKS = 4
+UNITS = 2 * E
+WORDS, BYTES_ = 0, 1
 
 
 def tile_moe_mmo_gelu_kernel(
@@ -32,6 +35,14 @@ def tile_moe_mmo_gelu_kernel(
         stage = ctx.enter_context(tc.tile_pool(name="stage", bufs=1))
         ring = ctx.enter_context(tc.tile_pool(name="ring", bufs=4))
         psum = ctx.enter_context(tc.psum_pool(name="psum", bufs=1))
+
+        def new_tile(shape, dtype, name, at):
+            if at is None:
+                return keep.tile(shape, dtype, name=name, align_bytes=64)
+            return stage.tile(shape, dtype, name=name, align_bytes=64, offset=at)
+
+        def slots_of(u):
+            return D if u < E else C
 
         def load_table(name, words, scales, lst, width, scale_queue):
             offsets = keep.tile([P, width // 16], U16, name=name + "_offsets")
@@ -66,9 +77,6 @@ def tile_moe_mmo_gelu_kernel(
             nc.sync.dma_start(g[:], gate)
             return g
 
-        def first_w(u):
-            return wz[u] if u < E else w1[u - E]
-
         z_lists = load_table("z", z_words, z_scales, offs2, Q, nc.scalar)
         load_half("first0", wz[0], 0)
         load_half("first0", wz[0], 1)
@@ -80,7 +88,7 @@ def tile_moe_mmo_gelu_kernel(
         gates = [load_gate("z_gate0", gate2[:, 0:D], D)[:]]
         for e in range(1, E):
             load_half("second%d" % e, w2[e], 0)
-            load_whole("first%d" % (e + 1), first_w(e + 1))
+            load_whole("first%d" % (e + 1), wz[e + 1] if e + 1 < E else w1[0])
             gates.append(load_gate("z_gate%d" % e, gate2[:, e * D : (e + 1) * D], D)[:])
             load_half("second%d" % e, w2[e], 1)
         load_whole("first5", w1[1])
@@ -89,23 +97,18 @@ def tile_moe_mmo_gelu_kernel(
         gates.extend([x_gate[:, e * C : (e + 1) * C] for e in range(E)])
         load_whole("first7", w1[3])
 
-        z_win = [keep.tile([P, Q], F32, name="z_win%d" % b) for b in range(4)]
-        x_win = [keep.tile([P, T], F32, name="x_win%d" % b) for b in range(4)]
+        z_win = [keep.tile([P, Q], F32, name="z_win%d" % b) for b in range(BLOCKS)]
+        x_win = [keep.tile([P, T], F32, name="x_win%d" % b) for b in range(BLOCKS)]
 
         tokens = {}
         first_q = {}
         second_q = {}
         hidden_q = {}
 
-        def new_tile(shape, dtype, name, at):
-            if at is None:
-                return keep.tile(shape, dtype, name=name, align_bytes=64)
-            return stage.tile(shape, dtype, name=name, align_bytes=64, offset=at)
-
         def gather(units, sort, at):
             offsets, table, plane = z_lists if units[0] < E else x_lists
-            window, dtype = (table[:].bitcast(U32), U32) if sort == 0 else (plane[:], U8)
-            slots = D if units[0] < E else C
+            window, dtype = (table[:].bitcast(U32), U32) if sort == WORDS else (plane[:], U8)
+            slots = slots_of(units[0])
             n = slots * len(units)
             s0 = (units[0] % E) * slots
             got = new_tile([P, n], dtype, "gathered%d_%d" % (sort, units[0]), at)
@@ -113,14 +116,10 @@ def tile_moe_mmo_gelu_kernel(
             for i, u in enumerate(units):
                 tokens[(u, sort)] = got[:, i * slots : (i + 1) * slots]
 
-        def quantise_first(u, at=None):
-            if at is None:
-                grouped = ring.tile([P, PACK, P, PACK], BF16, name="first_grouped", align_bytes=64, bufs=3)
-            else:
-                grouped = new_tile([P, PACK, P, PACK], BF16, "first_grouped_at", at)
+        def quantise_first(u, grouped):
             for h in range(2):
                 nc.scalar.copy(
-                    grouped[:, :, h * 64 : (h + 1) * 64, :].rearrange("p t m j -> p m j t"),
+                    grouped[:, :, h * P // 2 : (h + 1) * P // 2, :].rearrange("p t m j -> p m j t"),
                     raw[("first%d" % u, h)].rearrange("p j (m t) -> p m j t", t=PACK),
                 )
             codes = ring.tile([P, H], U32, name="first_codes", align_bytes=64)
@@ -128,11 +127,7 @@ def tile_moe_mmo_gelu_kernel(
             nc.vector.quantize_mx(out=codes[:].bitcast(FP8X4), scales=scales[:], in_=grouped[:].rearrange("p t m j -> p (t m j)"))
             first_q[u] = (codes, scales)
 
-        def quantise_second(e, h, cast=nc.scalar.copy, at=None):
-            if at is None:
-                grouped = ring.tile([P, HALF, PACK], BF16, name="second_grouped", align_bytes=64)
-            else:
-                grouped = new_tile([P, HALF, PACK], BF16, "second_grouped_at", at)
+        def quantise_second(e, h, cast, grouped):
             cast(
                 grouped[:].rearrange("p (c i) j -> p c j i", i=4),
                 raw[("second%d" % e, h)].rearrange("p j (c i) -> p c j i", i=4),
@@ -142,9 +137,14 @@ def tile_moe_mmo_gelu_kernel(
             nc.vector.quantize_mx(out=codes[:].bitcast(FP8X4), scales=scales[:], in_=grouped[:].rearrange("p c j -> p (c j)"))
             second_q[(e, h)] = (codes, scales)
 
+        def next_first(u):
+            quantise_first(u, ring.tile([P, PACK, P, PACK], BF16, name="first_grouped", align_bytes=64, bufs=3))
+
+        def next_second(e, h):
+            quantise_second(e, h, nc.scalar.copy, ring.tile([P, HALF, PACK], BF16, name="second_grouped", align_bytes=64))
+
         def hidden(u, banks, at):
-            slots = D if u < E else C
-            codes, bytes_ = tokens[(u, 0)], tokens[(u, 1)]
+            slots = slots_of(u)
             w_codes, w_scales = first_q[u]
             grouped = new_tile([P, slots, PACK], BF16, "hidden_grouped%d" % u, at)
             for g in range(slots // P):
@@ -155,8 +155,8 @@ def tile_moe_mmo_gelu_kernel(
                         out=acc[:, t, :],
                         lhsT=w_codes[:, t * P : (t + 1) * P].bitcast(FP8X4),
                         lhsT_scale=w_scales[:, t * P : (t + 1) * P],
-                        rhs=codes[:, cols].bitcast(FP8X4),
-                        rhs_scale=bytes_[:, cols],
+                        rhs=tokens[(u, WORDS)][:, cols].bitcast(FP8X4),
+                        rhs_scale=tokens[(u, BYTES_)][:, cols],
                         start=True,
                         stop=True,
                     )
@@ -168,10 +168,8 @@ def tile_moe_mmo_gelu_kernel(
 
         def results(u, blocks, bank, at):
             e = u % E
-            slots = D if u < E else C
-            offsets = (z_lists if u < E else x_lists)[0]
-            win = z_win if u < E else x_win
-            col0 = T if u < E else 0
+            slots = slots_of(u)
+            offsets, win, col0 = (z_lists[0], z_win, T) if u < E else (x_lists[0], x_win, 0)
             h_codes, h_scales = hidden_q[u]
             acc = psum.tile([P, len(blocks), slots], F32, name="second_acc%d_%d" % (u, blocks[0]), offset=bank * BANK)
             for i, nb in enumerate(blocks):
@@ -194,35 +192,42 @@ def tile_moe_mmo_gelu_kernel(
                 if e == E - 1:
                     nc.sync.dma_start(out[nb * P : (nb + 1) * P, col0 : col0 + E * slots], win[nb][:])
 
-        gather([0, 1], 0, None)
-        gather([2, 3], 0, None)
-        gather([0, 1, 2], 1, None)
-        quantise_first(0, len(place) * SLOT)
-        gather([3], 1, place[("first0", 1)])
-        quantise_second(0, 0, nc.vector.tensor_copy, len(place) * SLOT)
-        gather([4, 5], 0, place[("first0", 1)] + 1024)
-        gather([4, 5], 1, place[("first0", 1)] + 2048)
+        after_first0 = place[("first0", 1)]
+        after_first1 = place[("first1", 1)]
+        pair_words = 2 * C * 4
+        spare = len(place) * SLOT
+        gather([0, 1], WORDS, None)
+        gather([2, 3], WORDS, None)
+        gather([0, 1, 2], BYTES_, None)
+        quantise_first(0, new_tile([P, PACK, P, PACK], BF16, "first_grouped0", spare))
+        gather([3], BYTES_, after_first0)
+        quantise_second(0, 0, nc.vector.tensor_copy, new_tile([P, HALF, PACK], BF16, "second_grouped0", spare))
+        gather([4, 5], WORDS, after_first0 + pair_words)
+        gather([4, 5], BYTES_, after_first0 + 2 * pair_words)
         hidden(0, (0, 1), None)
-        quantise_first(1)
-        gather([6, 7], 0, place[("first1", 1)])
-        gather([6, 7], 1, place[("first1", 1)] + 1024)
-        quantise_second(0, 1)
+        next_first(1)
+        gather([6, 7], WORDS, after_first1)
+        gather([6, 7], BYTES_, after_first1 + pair_words)
+        next_second(0, 1)
+
         for u in range(E):
-            behind = place[("second%d" % u, 1)]
-            results(u, (0, 1), 4 + 2 * (u % 2), behind)
-            hidden(u + 1, (2, 3) if u % 2 == 0 else (0, 1), behind + SLOT // 2)
+            results(u, (0, 1), 4 + 2 * (u % 2), place[("second%d" % u, 1)])
             if u + 1 < E:
-                quantise_second(u + 1, 0)
-                results(u, (2, 3), 5 + 2 * (u % 2), place[("second%d" % (u + 1), 0)])
-                quantise_first(u + 2)
-                quantise_second(u + 1, 1)
+                next_second(u + 1, 0)
+                freed = place[("second%d" % (u + 1), 0)]
             else:
-                quantise_first(u + 2)
-                results(u, (2, 3), 5 + 2 * (u % 2), place[("first%d" % (u + 2), 0)])
-        for u in range(E, 2 * E):
+                next_first(u + 2)
+                freed = place[("first%d" % (u + 2), 0)]
+            hidden(u + 1, (2, 3) if u % 2 == 0 else (0, 1), freed + SLOT // 2)
+            results(u, (2, 3), 5 + 2 * (u % 2), freed)
+            if u + 1 < E:
+                next_first(u + 2)
+                next_second(u + 1, 1)
+
+        for u in range(E, UNITS):
             bank = 2 * ((u + 1) % 2)
-            if u + 1 < 2 * E:
+            if u + 1 < UNITS:
                 hidden(u + 1, (bank,), None)
-            if u + 2 < 2 * E:
-                quantise_first(u + 2)
-            results(u, (0, 1, 2, 3), bank, place[("first%d" % (u + 2), 0)] if u + 2 < 2 * E else None)
+            if u + 2 < UNITS:
+                next_first(u + 2)
+            results(u, tuple(range(BLOCKS)), bank, place[("first%d" % (u + 2), 0)] if u + 2 < UNITS else None)

from contextlib import ExitStack

import concourse.mybir as mybir

T, Q, E, C, D = 512, 1024, 4, 128, 256
H = 512
FLOPS = 2 * 2 * 512 * 512 * (T + Q)

F32 = mybir.dt.float32
BF16 = mybir.dt.bfloat16
I32 = mybir.dt.int32
U32 = mybir.dt.uint32
U16 = mybir.dt.uint16
U8 = mybir.dt.uint8
FP8X4 = mybir.dt.float8_e4m3fn_x4
MULT = mybir.AluOpType.mult
GELU = mybir.ActivationFunctionType.Gelu_apprx_tanh

P = 128
PACK = 4
HALF = 256
SLOT = PACK * HALF * 4
BANK = 2048
BLOCKS = 4
UNITS = 2 * E
WORDS, BYTES_ = 0, 1


def tile_moe_mmo_gelu_kernel(
    tc, x_words, x_scales, z_words, z_scales, w1, wz, w2, gate1, gate2, offs, offs2, out
):
    nc = tc.nc
    with ExitStack() as ctx:
        keep = ctx.enter_context(tc.tile_pool(name="keep", bufs=1))
        stage = ctx.enter_context(tc.tile_pool(name="stage", bufs=1))
        ring = ctx.enter_context(tc.tile_pool(name="ring", bufs=4))
        psum = ctx.enter_context(tc.psum_pool(name="psum", bufs=1))

        def new_tile(shape, dtype, name, at):
            if at is None:
                return keep.tile(shape, dtype, name=name, align_bytes=64)
            return stage.tile(shape, dtype, name=name, align_bytes=64, offset=at)

        def slots_of(u):
            return D if u < E else C

        def load_table(name, words, scales, lst, width, scale_queue):
            offsets = keep.tile([P, width // 16], U16, name=name + "_offsets")
            table = keep.tile([P, width], I32, name=name + "_table", align_bytes=64)
            plane = keep.tile([P, width], U8, name=name + "_plane", align_bytes=64)
            nc.vector.memset(plane[:].bitcast(I32), 0)
            nc.sync.dma_start(offsets[:], lst)
            nc.sync.dma_start(table[:], words[0].rearrange("p t d -> p (t d)").bitcast(I32))
            for r in range(4):
                scale_queue.dma_start(plane[r:P:32, :].bitcast(I32), scales[0, r:16:4, :].bitcast(I32))
            return offsets, table, plane

        raw = {}
        place = {}

        def load_half(key, w, h):
            place[(key, h)] = len(place) * SLOT
            t = stage.tile([P, PACK, HALF], F32, name="raw_%s%d" % (key, h), offset=place[(key, h)])
            nc.sync.dma_start(t[:], w[:, h * HALF : (h + 1) * HALF].rearrange("(p j) c -> p j c", j=PACK))
            raw[(key, h)] = t[:]

        def load_whole(key, w):
            for h in range(2):
                place[(key, h)] = len(place) * SLOT
            t = stage.tile([P, PACK, 2 * HALF], F32, name="raw_" + key, offset=place[(key, 0)])
            nc.sync.dma_start(t[:], w.rearrange("(p j) c -> p j c", j=PACK))
            for h in range(2):
                raw[(key, h)] = t[:, :, h * HALF : (h + 1) * HALF]

        def load_gate(name, gate, width):
            g = keep.tile([P, width], F32, name=name)
            nc.sync.dma_start(g[:], gate)
            return g

        z_lists = load_table("z", z_words, z_scales, offs2, Q, nc.scalar)
        load_half("first0", wz[0], 0)
        load_half("first0", wz[0], 1)
        load_half("first1", wz[1], 0)
        load_half("second0", w2[0], 0)
        x_lists = load_table("x", x_words, x_scales, offs, T, nc.sync)
        load_half("first1", wz[1], 1)
        load_half("second0", w2[0], 1)
        gates = [load_gate("z_gate0", gate2[:, 0:D], D)[:]]
        for e in range(1, E):
            load_half("second%d" % e, w2[e], 0)
            load_whole("first%d" % (e + 1), wz[e + 1] if e + 1 < E else w1[0])
            gates.append(load_gate("z_gate%d" % e, gate2[:, e * D : (e + 1) * D], D)[:])
            load_half("second%d" % e, w2[e], 1)
        load_whole("first5", w1[1])
        load_whole("first6", w1[2])
        x_gate = load_gate("x_gate", gate1, T)
        gates.extend([x_gate[:, e * C : (e + 1) * C] for e in range(E)])
        load_whole("first7", w1[3])

        z_win = [keep.tile([P, Q], F32, name="z_win%d" % b) for b in range(BLOCKS)]
        x_win = [keep.tile([P, T], F32, name="x_win%d" % b) for b in range(BLOCKS)]

        tokens = {}
        first_q = {}
        second_q = {}
        hidden_q = {}

        def gather(units, sort, at):
            offsets, table, plane = z_lists if units[0] < E else x_lists
            window, dtype = (table[:].bitcast(U32), U32) if sort == WORDS else (plane[:], U8)
            slots = slots_of(units[0])
            n = slots * len(units)
            s0 = (units[0] % E) * slots
            got = new_tile([P, n], dtype, "gathered%d_%d" % (sort, units[0]), at)
            nc.vector.tensor_copy(got[:], window.indirect(offsets[:, s0 // 16 : (s0 + n) // 16]))
            for i, u in enumerate(units):
                tokens[(u, sort)] = got[:, i * slots : (i + 1) * slots]

        def quantise_first(u, grouped):
            for h in range(2):
                nc.scalar.copy(
                    grouped[:, :, h * P // 2 : (h + 1) * P // 2, :].rearrange("p t m j -> p m j t"),
                    raw[("first%d" % u, h)].rearrange("p j (m t) -> p m j t", t=PACK),
                )
            codes = ring.tile([P, H], U32, name="first_codes", align_bytes=64)
            scales = ring.tile([P, H], U8, name="first_scales", align_bytes=64)
            nc.vector.quantize_mx(out=codes[:].bitcast(FP8X4), scales=scales[:], in_=grouped[:].rearrange("p t m j -> p (t m j)"))
            first_q[u] = (codes, scales)

        def quantise_second(e, h, cast, grouped):
            cast(
                grouped[:].rearrange("p (c i) j -> p c j i", i=4),
                raw[("second%d" % e, h)].rearrange("p j (c i) -> p c j i", i=4),
            )
            codes = keep.tile([P, HALF], U32, name="second_codes%d_%d" % (e, h), align_bytes=64)
            scales = keep.tile([P, HALF], U8, name="second_scales%d_%d" % (e, h), align_bytes=64)
            nc.vector.quantize_mx(out=codes[:].bitcast(FP8X4), scales=scales[:], in_=grouped[:].rearrange("p c j -> p (c j)"))
            second_q[(e, h)] = (codes, scales)

        def next_first(u):
            quantise_first(u, ring.tile([P, PACK, P, PACK], BF16, name="first_grouped", align_bytes=64, bufs=3))

        def next_second(e, h):
            quantise_second(e, h, nc.scalar.copy, ring.tile([P, HALF, PACK], BF16, name="second_grouped", align_bytes=64))

        def hidden(u, banks, at):
            slots = slots_of(u)
            w_codes, w_scales = first_q[u]
            grouped = new_tile([P, slots, PACK], BF16, "hidden_grouped%d" % u, at)
            for g in range(slots // P):
                acc = psum.tile([P, PACK, P], F32, name="first_acc%d_%d" % (u, g), offset=banks[g] * BANK)
                cols = slice(g * P, (g + 1) * P)
                for t in range(PACK):
                    nc.tensor.matmul_mx(
                        out=acc[:, t, :],
                        lhsT=w_codes[:, t * P : (t + 1) * P].bitcast(FP8X4),
                        lhsT_scale=w_scales[:, t * P : (t + 1) * P],
                        rhs=tokens[(u, WORDS)][:, cols].bitcast(FP8X4),
                        rhs_scale=tokens[(u, BYTES_)][:, cols],
                        start=True,
                        stop=True,
                    )
                nc.scalar.activation(grouped[:, cols, :], acc[:].rearrange("p t s -> p s t"), GELU)
            h_codes = ring.tile([P, slots], U32, name="hidden_codes", align_bytes=64)
            h_scales = ring.tile([P, slots], U8, name="hidden_scales", align_bytes=64)
            nc.vector.quantize_mx(out=h_codes[:].bitcast(FP8X4), scales=h_scales[:], in_=grouped[:].rearrange("p s t -> p (s t)"))
            hidden_q[u] = (h_codes, h_scales)

        def results(u, blocks, bank, at):
            e = u % E
            slots = slots_of(u)
            offsets, win, col0 = (z_lists[0], z_win, T) if u < E else (x_lists[0], x_win, 0)
            h_codes, h_scales = hidden_q[u]
            acc = psum.tile([P, len(blocks), slots], F32, name="second_acc%d_%d" % (u, blocks[0]), offset=bank * BANK)
            for i, nb in enumerate(blocks):
                w_codes, w_scales = second_q[(e, nb // 2)]
                cols = slice((nb % 2) * P, (nb % 2 + 1) * P)
                nc.tensor.matmul_mx(
                    out=acc[:, i, :],
                    lhsT=w_codes[:, cols].bitcast(FP8X4),
                    lhsT_scale=w_scales[:, cols],
                    rhs=h_codes[:].bitcast(FP8X4),
                    rhs_scale=h_scales[:],
                    start=True,
                    stop=True,
                )
            res = new_tile([P, len(blocks) * slots], F32, "res%d_%d" % (u, blocks[0]), at)
            nc.scalar.copy(res[:], acc[:].rearrange("p b s -> p (b s)"))
            lst = offsets[:, e * slots // 16 : (e + 1) * slots // 16]
            for i, nb in enumerate(blocks):
                nc.vector.tensor_tensor(win[nb][:].indirect(lst), res[:, i * slots : (i + 1) * slots], gates[u], MULT)
                if e == E - 1:
                    nc.sync.dma_start(out[nb * P : (nb + 1) * P, col0 : col0 + E * slots], win[nb][:])

        after_first0 = place[("first0", 1)]
        after_first1 = place[("first1", 1)]
        pair_words = 2 * C * 4
        spare = len(place) * SLOT
        gather([0, 1], WORDS, None)
        gather([2, 3], WORDS, None)
        gather([0, 1, 2], BYTES_, None)
        quantise_first(0, new_tile([P, PACK, P, PACK], BF16, "first_grouped0", spare))
        gather([3], BYTES_, after_first0)
        quantise_second(0, 0, nc.vector.tensor_copy, new_tile([P, HALF, PACK], BF16, "second_grouped0", spare))
        gather([4, 5], WORDS, after_first0 + pair_words)
        gather([4, 5], BYTES_, after_first0 + 2 * pair_words)
        hidden(0, (0, 1), None)
        next_first(1)
        gather([6, 7], WORDS, after_first1)
        gather([6, 7], BYTES_, after_first1 + pair_words)
        next_second(0, 1)

        for u in range(E):
            results(u, (0, 1), 4 + 2 * (u % 2), place[("second%d" % u, 1)])
            if u + 1 < E:
                next_second(u + 1, 0)
                freed = place[("second%d" % (u + 1), 0)]
            else:
                next_first(u + 2)
                freed = place[("first%d" % (u + 2), 0)]
            hidden(u + 1, (2, 3) if u % 2 == 0 else (0, 1), freed + SLOT // 2)
            results(u, (2, 3), 5 + 2 * (u % 2), freed)
            if u + 1 < E:
                next_first(u + 2)
                next_second(u + 1, 1)

        for u in range(E, UNITS):
            bank = 2 * ((u + 1) % 2)
            if u + 1 < UNITS:
                hidden(u + 1, (bank,), None)
            if u + 2 < UNITS:
                next_first(u + 2)
            results(u, tuple(range(BLOCKS)), bank, place[("first%d" % (u + 2), 0)] if u + 2 < UNITS else None)
